import numpy as np
import ml_dtypes

BF16 = ml_dtypes.bfloat16


def bf(x):
    return np.asarray(x, np.float32).astype(BF16)


def f32(x):
    return np.asarray(x, np.float32)


def f64(x):
    return np.asarray(x).astype(np.float64)


def striped(idx):
    return np.tile(idx.reshape(-1, 16).T, (8, 1))


def rows(idx, k):
    return np.tile(idx, (k, 1))


def look(tab, idx):
    return np.take_along_axis(f64(tab), rows(idx, len(tab)), axis=1)


K, S, V, N = 256, 256, 256, 256


def setup_inputs():
    return {"tab": bf(0.5 * np.random.standard_normal((K, S))), "y": f32(np.random.standard_normal((K, V))), "offs": striped(np.random.permutation(S)[:N])}


def reference(tab, y, offs):
    idx = offs[:16].T.reshape(-1)
    t = look(tab, idx)
    x = np.exp(t) * f64(y)
    return x

@@ -1,0 +1,42 @@
+import concourse.mybir as mybir
+
+BF16, F32, U16 = mybir.dt.bfloat16, mybir.dt.float32, mybir.dt.uint16
+EXP = mybir.ActivationFunctionType.Exp
+MULT = mybir.AluOpType.mult
+
+P = 128
+ROWS, COLS, N = 256, 256, 256
+BLOCKS = ROWS // P
+PIECE = N // 2
+PER_COLUMN = 16
+
+
+def tile_lookup_gate_exp_out_kernel(tc, tab, y, offs, out):
+    nc = tc.nc
+    with tc.tile_pool(name="held", bufs=1) as held:
+        offsets = held.tile([P, N // PER_COLUMN], U16, name="offsets")
+        nc.sync.dma_start(offsets[:], offs)
+        tables = []
+        for b in range(BLOCKS):
+            table = held.tile([P, COLS], BF16, name=f"table{b}")
+            nc.sync.dma_start(table[:], tab[b * P : (b + 1) * P, :])
+            tables.append(table)
+        streams = []
+        for b in range(BLOCKS):
+            stream = held.tile([P, N], F32, name=f"stream{b}")
+            nc.sync.dma_start(stream[:], y[b * P : (b + 1) * P, :])
+            streams.append(stream)
+
+        for b in range(BLOCKS):
+            gates = held.tile([P, N], F32, name=f"gates{b}")
+            products = held.tile([P, N], F32, name=f"products{b}")
+            for start in range(0, N, PIECE):
+                entries = slice(start, start + PIECE)
+                columns = slice(start // PER_COLUMN, (start + PIECE) // PER_COLUMN)
+                nc.scalar.activation(
+                    gates[:, entries], tables[b][:].indirect(offsets[:, columns]), EXP
+                )
+                nc.vector.tensor_tensor(
+                    products[:, entries], gates[:, entries], streams[b][:, entries], MULT
+                )
+            nc.sync.dma_start(out[b * P : (b + 1) * P, :], products[:])

@@ -14,6 +14,11 @@ PER_COLUMN = 16
 def tile_lookup_gate_exp_out_kernel(tc, tab, y, offs, out):
     nc = tc.nc
     with tc.tile_pool(name="held", bufs=1) as held:
+        warm = held.tile([P, 1], F32, name="warm")
+        nc.vector.memset(warm[:], 0.0)
+        warmed = held.tile([P, 1], F32, name="warmed")
+        nc.scalar.activation(warmed[:], warm[:], EXP)
+
         offsets = held.tile([P, N // PER_COLUMN], U16, name="offsets")
         nc.sync.dma_start(offsets[:], offs)
         tables = []

@@ -14,18 +14,18 @@ PER_COLUMN = 16
 def tile_lookup_gate_exp_out_kernel(tc, tab, y, offs, out):
     nc = tc.nc
     with tc.tile_pool(name="held", bufs=1) as held:
-        warm = held.tile([P, 1], F32, name="warm")
-        nc.vector.memset(warm[:], 0.0)
-        warmed = held.tile([P, 1], F32, name="warmed")
-        nc.scalar.activation(warmed[:], warm[:], EXP)
-
         offsets = held.tile([P, N // PER_COLUMN], U16, name="offsets")
         nc.sync.dma_start(offsets[:], offs)
         tables = []
         for b in range(BLOCKS):
             table = held.tile([P, COLS], BF16, name=f"table{b}")
-            nc.sync.dma_start(table[:], tab[b * P : (b + 1) * P, :])
+            nc.scalar.dma_start(table[:], tab[b * P : (b + 1) * P, :])
             tables.append(table)
+        warm = held.tile([P, 1], F32, name="warm")
+        nc.vector.memset(warm[:], 0.0)
+        warmed = held.tile([P, 1], F32, name="warmed")
+        nc.scalar.activation(warmed[:], warm[:], EXP)
+
         streams = []
         for b in range(BLOCKS):
             stream = held.tile([P, N], F32, name=f"stream{b}")

@@ -14,23 +14,22 @@ PER_COLUMN = 16
 def tile_lookup_gate_exp_out_kernel(tc, tab, y, offs, out):
     nc = tc.nc
     with tc.tile_pool(name="held", bufs=1) as held:
-        offsets = held.tile([P, N // PER_COLUMN], U16, name="offsets")
-        nc.sync.dma_start(offsets[:], offs)
-        tables = []
-        for b in range(BLOCKS):
-            table = held.tile([P, COLS], BF16, name=f"table{b}")
-            nc.scalar.dma_start(table[:], tab[b * P : (b + 1) * P, :])
-            tables.append(table)
         warm = held.tile([P, 1], F32, name="warm")
         nc.vector.memset(warm[:], 0.0)
         warmed = held.tile([P, 1], F32, name="warmed")
         nc.scalar.activation(warmed[:], warm[:], EXP)
 
-        streams = []
+        offsets = held.tile([P, N // PER_COLUMN], U16, name="offsets")
+        nc.sync.dma_start(offsets[:], offs)
+        tab_blocks = tab.rearrange("(p b) n -> p b n", b=BLOCKS)
+        out_blocks = out.rearrange("(p b) n -> p b n", b=BLOCKS)
+        tables = []
         for b in range(BLOCKS):
-            stream = held.tile([P, N], F32, name=f"stream{b}")
-            nc.sync.dma_start(stream[:], y[b * P : (b + 1) * P, :])
-            streams.append(stream)
+            table = held.tile([P, COLS], BF16, name=f"table{b}")
+            nc.sync.dma_start(table[:], tab_blocks[:, b, :])
+            tables.append(table)
+        streams = held.tile([P, BLOCKS, N], F32, name="streams")
+        nc.sync.dma_start(streams[:], y.rearrange("(p b) n -> p b n", b=BLOCKS))
 
         for b in range(BLOCKS):
             gates = held.tile([P, N], F32, name=f"gates{b}")
@@ -42,6 +41,6 @@ def tile_lookup_gate_exp_out_kernel(tc, tab, y, offs, out):
                     gates[:, entries], tables[b][:].indirect(offsets[:, columns]), EXP
                 )
                 nc.vector.tensor_tensor(
-                    products[:, entries], gates[:, entries], streams[b][:, entries], MULT
+                    products[:, entries], gates[:, entries], streams[:, b, entries], MULT
                 )
-            nc.sync.dma_start(out[b * P : (b + 1) * P, :], products[:])
+            nc.sync.dma_start(out_blocks[:, b, :], products[:])

import concourse.mybir as mybir

BF16, F32, U16 = mybir.dt.bfloat16, mybir.dt.float32, mybir.dt.uint16
EXP = mybir.ActivationFunctionType.Exp
MULT = mybir.AluOpType.mult

P = 128
ROWS, COLS, N = 256, 256, 256
BLOCKS = ROWS // P
PIECE = N // 2
PER_COLUMN = 16


def tile_lookup_gate_exp_out_kernel(tc, tab, y, offs, out):
    nc = tc.nc
    with tc.tile_pool(name="held", bufs=1) as held:
        warm = held.tile([P, 1], F32, name="warm")
        nc.vector.memset(warm[:], 0.0)
        warmed = held.tile([P, 1], F32, name="warmed")
        nc.scalar.activation(warmed[:], warm[:], EXP)

        offsets = held.tile([P, N // PER_COLUMN], U16, name="offsets")
        nc.sync.dma_start(offsets[:], offs)
        tab_blocks = tab.rearrange("(p b) n -> p b n", b=BLOCKS)
        out_blocks = out.rearrange("(p b) n -> p b n", b=BLOCKS)
        tables = []
        for b in range(BLOCKS):
            table = held.tile([P, COLS], BF16, name=f"table{b}")
            nc.sync.dma_start(table[:], tab_blocks[:, b, :])
            tables.append(table)
        streams = held.tile([P, BLOCKS, N], F32, name="streams")
        nc.sync.dma_start(streams[:], y.rearrange("(p b) n -> p b n", b=BLOCKS))

        for b in range(BLOCKS):
            gates = held.tile([P, N], F32, name=f"gates{b}")
            products = held.tile([P, N], F32, name=f"products{b}")
            for start in range(0, N, PIECE):
                entries = slice(start, start + PIECE)
                columns = slice(start // PER_COLUMN, (start + PIECE) // PER_COLUMN)
                nc.scalar.activation(
                    gates[:, entries], tables[b][:].indirect(offsets[:, columns]), EXP
                )
                nc.vector.tensor_tensor(
                    products[:, entries], gates[:, entries], streams[:, b, entries], MULT
                )
            nc.sync.dma_start(out_blocks[:, b, :], products[:])
